import numpy as np, ml_dtypes
CORES = [3,1,0,2]
N = 4
def setup_inputs(rng):
    return {"x": rng.standard_normal((N, 128, 2048), dtype=np.float32).astype(ml_dtypes.bfloat16)}
def reference(x):
    p = 128 // N
    blocks = x.reshape(N, N, p, 2048)
    return {"y": np.ascontiguousarray(blocks.transpose(1, 0, 2, 3)).reshape(N, 128, 2048)}

@@ -1,0 +1,48 @@
+from concourse.bass import DstId, RemoteDMATransfer
+
+N = 4
+P = 128 // N
+W = 2048 // N
+
+SCRATCH = {
+    "send": ("dram", [N, 128, W], "bfloat16"),
+    "land": ("dram", [N, 128, W], "bfloat16"),
+}
+SEMAPHORES = ["loaded", "read", "arrived", "stored"]
+
+
+def runs(idx):
+    out = []
+    for j in idx:
+        if out and out[-1][1] == j:
+            out[-1][1] = j + 1
+        else:
+            out.append([j, j + 1])
+    return out
+
+
+def rank_program(g, core, T, topo):
+    r = T.rank_of(core)
+    if r is None:
+        return
+    others = [j for j in range(N) if j != r]
+    pieces = runs(others)
+
+    for a, b in pieces:
+        g.dma_start(T.send[a:b], T.x[a * P:b * P, :]).then_inc(T.sem.loaded, 16)
+    g.dma_start(T.y[r * P:(r + 1) * P, :], T.x[r * P:(r + 1) * P, :]).then_inc(T.sem.stored, 16)
+    g.wait_ge(T.sem.loaded, 16 * len(pieces))
+
+    transfers = []
+    for k, j in enumerate(others):
+        rid, pid, _se = topo.addr(T.cores[j])
+        transfers.append(RemoteDMATransfer(
+            dst_ids=[DstId(rid=rid, pnc=pid)], dma_engine_mask=0xF << (4 * k), remote_sem=T.sem.arrived,
+            src=T.send[j], dst=T.land[r]))
+    g.remote_dma_fused(transfers, local_sem=T.sem.read)
+
+    g.wait_ge(T.sem.arrived, 4 * len(others))
+    for a, b in pieces:
+        g.dma_start(T.y[a * P:b * P, :], T.land[a:b]).then_inc(T.sem.stored, 16)
+    g.wait_ge(T.sem.stored, 16 * (len(pieces) + 1))
+    g.wait_ge(T.sem.read, 4 * len(others))

@@ -1,48 +1,35 @@
 from concourse.bass import DstId, RemoteDMATransfer
 
 N = 4
-P = 128 // N
 W = 2048 // N
+STEP = N
+SLOTS = STEP * (N - 1) + 1
 
 SCRATCH = {
-    "send": ("dram", [N, 128, W], "bfloat16"),
-    "land": ("dram", [N, 128, W], "bfloat16"),
+    "buf": ("dram", [SLOTS, 128, W], "bfloat16"),
 }
 SEMAPHORES = ["loaded", "read", "arrived", "stored"]
-
-
-def runs(idx):
-    out = []
-    for j in idx:
-        if out and out[-1][1] == j:
-            out[-1][1] = j + 1
-        else:
-            out.append([j, j + 1])
-    return out
 
 
 def rank_program(g, core, T, topo):
     r = T.rank_of(core)
     if r is None:
         return
-    others = [j for j in range(N) if j != r]
-    pieces = runs(others)
+    first = (STEP - 1) * r
+    peers = [j for j in range(N) if j != r]
 
-    for a, b in pieces:
-        g.dma_start(T.send[a:b], T.x[a * P:b * P, :]).then_inc(T.sem.loaded, 16)
-    g.dma_start(T.y[r * P:(r + 1) * P, :], T.x[r * P:(r + 1) * P, :]).then_inc(T.sem.stored, 16)
-    g.wait_ge(T.sem.loaded, 16 * len(pieces))
+    g.dma_start(T.buf[first:first + N], T.x[:, :]).then_inc(T.sem.loaded, 16)
+    g.wait_ge(T.sem.loaded, 16)
 
     transfers = []
-    for k, j in enumerate(others):
-        rid, pid, _se = topo.addr(T.cores[j])
+    for k, j in enumerate(peers):
+        rid, pid, sengine = topo.addr(T.cores[j])
         transfers.append(RemoteDMATransfer(
             dst_ids=[DstId(rid=rid, pnc=pid)], dma_engine_mask=0xF << (4 * k), remote_sem=T.sem.arrived,
-            src=T.send[j], dst=T.land[r]))
+            src=T.buf[first + j], dst=T.buf[STEP * r]))
     g.remote_dma_fused(transfers, local_sem=T.sem.read)
 
-    g.wait_ge(T.sem.arrived, 4 * len(others))
-    for a, b in pieces:
-        g.dma_start(T.y[a * P:b * P, :], T.land[a:b]).then_inc(T.sem.stored, 16)
-    g.wait_ge(T.sem.stored, 16 * (len(pieces) + 1))
-    g.wait_ge(T.sem.read, 4 * len(others))
+    g.wait_ge(T.sem.arrived, 4 * len(peers))
+    g.dma_start(T.y[:, :], T.buf[0:SLOTS:STEP]).then_inc(T.sem.stored, 16)
+    g.wait_ge(T.sem.stored, 16)
+    g.wait_ge(T.sem.read, 4 * len(peers))

from concourse.bass import DstId, RemoteDMATransfer

N = 4
W = 2048 // N
STEP = N
SLOTS = STEP * (N - 1) + 1

SCRATCH = {
    "buf": ("dram", [SLOTS, 128, W], "bfloat16"),
}
SEMAPHORES = ["loaded", "read", "arrived", "stored"]


def rank_program(g, core, T, topo):
    r = T.rank_of(core)
    if r is None:
        return
    first = (STEP - 1) * r
    peers = [j for j in range(N) if j != r]

    g.dma_start(T.buf[first:first + N], T.x[:, :]).then_inc(T.sem.loaded, 16)
    g.wait_ge(T.sem.loaded, 16)

    transfers = []
    for k, j in enumerate(peers):
        rid, pid, sengine = topo.addr(T.cores[j])
        transfers.append(RemoteDMATransfer(
            dst_ids=[DstId(rid=rid, pnc=pid)], dma_engine_mask=0xF << (4 * k), remote_sem=T.sem.arrived,
            src=T.buf[first + j], dst=T.buf[STEP * r]))
    g.remote_dma_fused(transfers, local_sem=T.sem.read)

    g.wait_ge(T.sem.arrived, 4 * len(peers))
    g.dma_start(T.y[:, :], T.buf[0:SLOTS:STEP]).then_inc(T.sem.stored, 16)
    g.wait_ge(T.sem.stored, 16)
    g.wait_ge(T.sem.read, 4 * len(peers))
